import numpy as np
import ml_dtypes


def mxq(x, axis, fmt="e4m3"):
    dtype, down = {"e4m3": (ml_dtypes.float8_e4m3fn, 7), "e5m2": (ml_dtypes.float8_e5m2, 14)}[fmt]
    v = np.moveaxis(np.asarray(x, np.float32).astype(ml_dtypes.bfloat16).astype(np.float64), axis, -1)
    blocks = v.reshape(v.shape[:-1] + (-1, 32))
    amax = np.abs(blocks).max(-1, keepdims=True)
    byte = np.maximum(np.where(amax > 0, np.frexp(amax)[1] - 1 + 127, 0) - down, 1)
    scale = np.exp2(byte - 127.0)
    codes = (blocks / scale).astype(np.float32).astype(dtype).astype(np.float64)
    return np.moveaxis((codes * scale).reshape(v.shape), -1, axis)


WIDE = False


def mx_kscale(k):
    if not WIDE:
        return np.ones(k)
    levels = np.array([10, -10, 5, -5, 0])
    if k % 512:
        return np.exp2(np.random.permutation(np.resize(levels, k // 32))).repeat(32)
    a = np.empty((k // 512, 16))
    for p in range(k // 512):
        a[p, :8] = np.random.permutation(np.resize(levels, 8))
        for g in range(8):
            far = levels[np.abs(levels - a[p, g]) >= 10]
            a[p, g + 8] = far[np.random.randint(len(far))]
    return np.exp2(a.ravel()).repeat(32)


BF16 = ml_dtypes.bfloat16


def bf(x):
    return np.asarray(x, np.float32).astype(BF16)


def f64(x):
    return np.asarray(x).astype(np.float64)


E2M1 = np.array([0.0, 0.5, 1.0, 1.5, 2.0, 3.0, 4.0, 6.0, -0.0, -0.5, -1.0, -1.5, -2.0, -3.0, -4.0, -6.0])


def pack_weight(w, fmt):
    k, n = w.shape
    w = f64(bf(w)).reshape(k // 32, 32, n)
    amax = np.abs(w).max(1)
    if fmt == "e4m3":
        byte = np.frexp(amax)[1] - 1 + 127 - 7
    else:
        mant, ex = np.frexp(amax / 6.0)
        byte = np.where(mant > 0.5, ex, ex - 1) + 127
    byte = np.clip(np.where(amax > 0, byte, 1), 1, 254)
    scaled = (w * np.exp2(127.0 - byte)[:, None, :]).reshape(k, n).astype(np.float32)
    by_word = np.ascontiguousarray(scaled.reshape(k // 512, 128, 4, n).transpose(0, 1, 3, 2))
    if fmt == "e4m3":
        words = by_word.astype(ml_dtypes.float8_e4m3fn).view(np.uint8)
    else:
        c = by_word.astype(ml_dtypes.float4_e2m1fn).view(np.uint8) & 0xF
        words = c[..., 0::2] | (c[..., 1::2] << 4)
    return np.ascontiguousarray(words), np.ascontiguousarray(byte.astype(np.uint8).reshape(k // 512, 16, n))


def unpack_weight(words, scales, fmt):
    g, p, n, _ = words.shape
    if fmt == "e4m3":
        vals = np.ascontiguousarray(words).view(ml_dtypes.float8_e4m3fn).astype(np.float64)
    else:
        nib = np.empty((g, p, n, 4), np.uint8)
        nib[..., 0::2] = words & 0xF
        nib[..., 1::2] = words >> 4
        vals = E2M1[nib]
    vals = vals * np.repeat(np.exp2(scales.astype(np.float64) - 127.0), 8, axis=1)[..., None]
    return vals.transpose(0, 1, 3, 2).reshape(g * 512, n)
def pack4(w):
    words, scales = pack_weight(w, "e2m1")
    return words.reshape(words.shape[0], 128, -1), scales


def unpack4(words, scales):
    return unpack_weight(words.reshape(words.shape[0], 128, -1, 2), scales, "e2m1")


E4M3FN = np.array([(-1.0 if i & 128 else 1.0) * ((1.0 + (i & 7) / 8.0) * 2.0 ** (((i >> 3) & 15) - 7) if i & 120 else (i & 7) * 2.0 ** -9) for i in range(256)])


def e4m3fn_bytes(y):
    return np.clip(np.asarray(y, np.float64), -448.0, 448.0).astype(np.float32).astype(ml_dtypes.float8_e4m3fn).view(np.uint8)


def e4m3fn_values(b):
    return E4M3FN[b]


B, K, N, D, C, V = 2, 256, 1024, 512, 512, 512


def draw0():
    s, r, t = mx_kscale(D), mx_kscale(C), mx_kscale(N)
    c = bf(np.random.standard_normal((B, K, D)) * s)
    x = bf(np.random.standard_normal((B, N, D)) / s)
    b = bf(0.5 * np.random.standard_normal(K))
    f = bf(np.random.standard_normal((B, N, C)) * r[None, :] * t[:, None])
    wv_words, wv_scales = pack4(np.random.standard_normal((C, V)) / np.sqrt(C) / r[:, None])
    return {
        "c": c,
        "x": x,
        "b": b,
        "f": f,
        "wv_words": wv_words,
        "wv_scales": wv_scales,
        "g": bf(np.random.standard_normal(N) / t),
        "h": bf(np.random.standard_normal((B, K, V))),
    }


def assign_to_clusters(c, x, b):
    cq = mxq(f64(c), 2, "e4m3")
    xq = mxq(f64(x), 2, "e4m3")
    s = (cq @ xq.transpose(0, 2, 1)) / np.sqrt(D)
    s = s + f64(b)[None, :, None]
    e = np.exp(s - s.max(axis=1, keepdims=True))
    return e / e.sum(axis=1, keepdims=True)


def core(c, x, b, f, wv_words, wv_scales, g, h):
    p = assign_to_clusters(c, x, b)
    a = K * p * f64(g)[None, None, :]
    v = mxq(f64(f), 2, "e4m3") @ unpack4(wv_words, wv_scales)
    u = (mxq(a, 2, "e4m3") @ mxq(v, 1, "e4m3")) / np.sqrt(N)
    return f64(h) + u


def setup_inputs():
    drawn = draw0()
    full = np.asarray(drawn['x']).astype(np.float64)
    scale = (np.abs(full).reshape(2, 1024, 4, 128).max(axis=(3,)) / 448.0).astype(np.float32)
    given = {}
    for key, value in drawn.items():
        if key == 'x':
            given['x_bytes'] = e4m3fn_bytes(full / np.repeat(scale.astype(np.float64), 128, axis=2))
            given['x_scale'] = scale
        else:
            given[key] = value
    return given


def reference(c, x_bytes, x_scale, b, f, wv_words, wv_scales, g, h):
    return core(c, e4m3fn_values(x_bytes) * np.repeat(x_scale.astype(np.float64), 128, axis=2), b, f, wv_words, wv_scales, g, h)

from contextlib import ExitStack
import math

import concourse.mybir as mybir
from concourse.masks import make_identity

B, K, N, D, C, V = 2, 256, 1024, 512, 512, 512
FLOPS = 2 * B * N * (K * D + C * V + K * V)

F32 = mybir.dt.float32
BF16 = mybir.dt.bfloat16
U32 = mybir.dt.uint32
I32 = mybir.dt.int32
U8 = mybir.dt.uint8
FP8 = mybir.dt.float8_e4m3fn
FP8X4 = mybir.dt.float8_e4m3fn_x4
FP4X4 = mybir.dt.float4_e2m1fn_x4
ALU = mybir.AluOpType
ACT = mybir.ActivationFunctionType
AX = mybir.AxisListType

P = 128
UNITS = 4

ORDER = """
LS:d LX00:d LX01:d LX1:d LX2:d LC0:d LB:d LX3:d LF01:d LC1:d LF00:d LF3:d
LF1:d LW0:d LW1:d LW2:d LW3:d LG:d LWW:d LF2:d LH0:d LH1:d W01:v W00:s
W02:v TX00:p W03:v TX01:p W13:v W10:s W21:v W23:v W12:s W11:s TC0:p W20:v
TX11:p W22:v TB:p TX21:p CC0:v CX01:s TX20:p QX01:v CB:v CX00:s TX10:p CX11:s
W32:s QX00:v QC0:v W30:v W31:v CX21:s MS01:p W33:v MS00:p TF01:p TC1:p QX11:v
TF31:p CX20:s B00:v QX21:v CX10:s QX10:v TF00:p CF01:s B01:v X00:v CC1:s QF01:v
TF11:p X01:v MS10:p CF31:s CF00:s TF10:p QX20:v E01:s B10:v E00:s QC1:v MS11:p
QF00:v TX30:p CF11:s E03:s X10:v E02:s CF10:s TF21:p R0:v MV00:p QF11:v QF31:v
F0:v E11:s CV00:s MV03:p MS21:p MV01:p MS20:p QF10:v MV11:p B11:v B21:v TF30:p
X11:v TF20:p CF21:s E10:s CV11:s CX30:v X21:v CF30:s QF30:v MV02:p E13:s E12:s
CF20:s QX30:v A00:g A01:g MV12:p R1:v MV33:p MS30:p CV12:s TX31:p MV13:p E22:s
QF21:v CV01:s F1:v QF20:v B20:v B30:v X20:v X30:v CV02:s CX31:s E23:s MV20:p
A10:g E21:s CV03:v QX31:v QV00:v MV10:p E20:s QV01:v QA00:v MV23:p CV10:s MV21:p
R2:v QA01:v MS31:p QV10:v QA10:v F2:v A11:g QA11:v CV13:s MU01:p MU00:p E30:s
QV11:v CV20:s E31:s CV23:s A20:g B31:v MV22:p X31:v MU10:p MU11:p O00:v MV30:p
O01:v CV21:s E33:s E32:s MV31:p QV20:v R3:v A21:g CV22:s QA20:v ST00:d QA21:v
CV30:s MV32:p CV31:s ST01:d F3:v QV21:v MU21:p A30:v A31:v CV33:s MU20:p QV30:v
QA30:v CV32:s QV31:v QA31:v MU30:p MU31:p O100:v O110:v ST100:d O111:v O101:v ST110:d
ST111:d ST101:d
""".split()


def tile_clusterassigncenterupdate_d1p_kernel(tc, c, x_bytes, x_scale, b, f, wv_words, wv_scales, g, h, out):
    nc = tc.nc
    with ExitStack() as ctx:
        sb = ctx.enter_context(tc.tile_pool(name="sb", bufs=1))
        psum = ctx.enter_context(tc.psum_pool(name="psum", bufs=1))
        ctx.enter_context(tc.manual_schedule())

        def tiles(name, count, shape, dtype):
            return [sb.tile(shape, dtype, name="%s%d" % (name, n), align_bytes=64) for n in range(count)]

        ident = sb.tile([P, P], F32, name="ident", align_bytes=64)
        warm = sb.tile([P, 2], F32, name="warm", align_bytes=64)
        xs = sb.tile([P, UNITS, 16], F32, name="xs", align_bytes=64)
        bcol = sb.tile([P, 2], BF16, name="bcol", align_bytes=64)
        bias = sb.tile([P, K], F32, name="bias", align_bytes=64)
        gt = sb.tile([P, 2, 4], BF16, name="gt", align_bytes=64)
        wv = sb.tile([P, 2 * V], U8, name="wv", align_bytes=64)
        wvs = sb.tile([P, V], U8, name="wvs", align_bytes=64)
        xb = tiles("xbytes", UNITS, [P, 4 * D], U8)
        xw = tiles("xw", UNITS, [P, 4, D], BF16)
        xg = tiles("xg", UNITS, [P, 4 * 512], BF16)
        xc = tiles("xc", UNITS, [P, 512], U32)
        xsc = tiles("xsc", UNITS, [P, 512], U8)
        fr = tiles("fr", UNITS, [P, 4, C], BF16)
        fg = tiles("fg", UNITS, [P, 4 * 512], BF16)
        fc = tiles("fc", UNITS, [P, 512], U32)
        fsc = tiles("fsc", UNITS, [P, 512], U8)
        cr = tiles("cr", B, [P, 2, D], BF16)
        cg = tiles("cg", B, [P, 4 * K], BF16)
        cc = tiles("cc", B, [P, K], U32)
        csc = tiles("csc", B, [P, K], U8)
        ht = tiles("ht", B, [P, 2, V], BF16)
        tneg = tiles("tneg", UNITS, [P, 4, K], F32)
        mn = tiles("mn", UNITS, [P, 4], F32)
        ex = tiles("ex", UNITS, [P, 4, K], F32)
        sums = tiles("sums", UNITS, [P, 4], F32)
        rec = tiles("rec", UNITS, [P, 4], F32)
        fac = tiles("fac", UNITS, [P, 4], F32)
        ag = tiles("ag", UNITS, [P, 4 * K], BF16)
        ac = tiles("ac", UNITS, [P, K], U32)
        asc = tiles("asc", UNITS, [P, K], U8)
        vg = tiles("vg", UNITS, [P, 4 * V], BF16)
        vc = tiles("vc", UNITS, [P, V], U32)
        vsc = tiles("vsc", UNITS, [P, V], U8)
        ot = tiles("ot", 2 * B, [P, V], F32)

        free_banks = list(range(8))
        held = {}

        def take(key):
            k = free_banks[0]
            free_banks.remove(k)
            bank = psum.tile([P, 512], F32, name="bank%d" % k, tag="bank%d" % k)
            held[key] = (k, bank)
            return bank

        def give(key):
            k, bank = held[key]
            free_banks.append(k)
            return bank

        def copy(eng, dst, src):
            if eng == "s":
                nc.scalar.copy(out=dst, in_=src)
            else:
                nc.vector.tensor_copy(out=dst, in_=src)

        def turn(key, rows):
            bank = take(key)
            for r in range(2):
                words = rows[r].bitcast(F32)
                for u in range(2):
                    nc.tensor.transpose(bank[:, (2 * r + u) * P:(2 * r + u + 1) * P], words[:, u:2 * P:2], ident[:])

        def unturn(eng, key, dst):
            bank = give(key)
            copy(eng, dst.bitcast(F32).rearrange("p (r m u) -> p r m u", r=2, u=2), bank[:].rearrange("p (r u m) -> p r m u", r=2, u=2))

        def quant(codes, scales, src):
            nc.vector.quantize_mx(out=codes.bitcast(FP8X4), scales=scales, in_=src)

        def xrows(i):
            return x_bytes[i // 2].rearrange("(g p t) k -> g p (t k)", p=P, t=4)[i % 2]

        def frows(i):
            return f[i // 2].rearrange("(g p t) k -> g p t k", p=P, t=4)[i % 2]

        nc.vector.memset(warm[:, 0:1], 0.0)
        nc.vector.memset(wvs[:].bitcast(I32), 0)
        nc.scalar.activation(out=warm[:, 1:2], in_=warm[:, 0:1], func=ACT.Exp)
        make_identity(nc, ident[:])

        for step in ORDER:
            name, eng = step.split(":")
            kind = "".join(ch for ch in name if ch not in "0123456789")
            nums = [int(ch) for ch in name if ch in "0123456789"]
            i = nums[0] if nums else 0
            j = nums[1] if len(nums) > 1 else None
            if kind == "LS":
                nc.sync.dma_start(out=xs[:], in_=x_scale.rearrange("b (g p t) j -> p (b g) (t j)", p=P, t=4))
            elif kind == "LB":
                nc.sync.dma_start(out=bcol[:], in_=b.rearrange("(p j) -> p j", j=2))
            elif kind == "LG":
                nc.sync.dma_start(out=gt[:], in_=g.rearrange("(g p t) -> p g t", p=P, t=4))
            elif kind == "LWW":
                nc.sync.dma_start(out=wv[:].bitcast(I32), in_=wv_words[0].bitcast(I32))
            elif kind == "LW":
                nc.sync.dma_start(out=wvs[32 * i:32 * i + 4, :].bitcast(I32), in_=wv_scales[0, 4 * i:4 * i + 4, :].bitcast(I32))
            elif kind == "LX":
                cols = slice(0, 4 * D) if j is None else slice(2 * D * j, 2 * D * (j + 1))
                nc.sync.dma_start(out=xb[i][:, cols], in_=xrows(i)[:, cols])
            elif kind == "LF":
                ts = slice(0, 4) if j is None else slice(2 * j, 2 * j + 2)
                nc.sync.dma_start(out=fr[i][:, ts, :], in_=frows(i)[:, ts, :])
            elif kind == "LC":
                nc.sync.dma_start(out=cr[i][:], in_=c[i].rearrange("(m j) k -> m j k", j=2))
            elif kind == "LH":
                nc.sync.dma_start(out=ht[i][:], in_=h[i].rearrange("(m j) k -> m j k", j=2))
            elif kind == "TB":
                bank = take("b")
                nc.tensor.transpose(bank[:, 0:P], bcol[:].bitcast(F32).to_broadcast([P, P]), ident[:])
            elif kind == "CB":
                bank = give("b")
                nc.vector.tensor_copy(out=bias[:].rearrange("p (j m) -> p j m", j=2), in_=bank[:, 0:P].bitcast(BF16).rearrange("p (m j) -> p j m", j=2))
            elif kind == "TC":
                turn(("c", i), [cr[i][:, 0, :], cr[i][:, 1, :]])
            elif kind == "CC":
                unturn(eng, ("c", i), cg[i][:])
            elif kind == "QC":
                quant(cc[i][:], csc[i][:], cg[i][:])
            elif kind == "W":
                for q in range(4):
                    src = xb[i][:, j * D + q * P:j * D + (q + 1) * P].bitcast(FP8)
                    dst = xw[i][:, j, q * P:(q + 1) * P]
                    scale = xs[:, i, 4 * j + q:4 * j + q + 1]
                    if eng == "s":
                        nc.scalar.activation(out=dst, in_=src, func=ACT.Copy, scale=scale)
                    else:
                        nc.vector.tensor_scalar(out=dst, in0=src, scalar1=scale, scalar2=None, op0=ALU.mult)
            elif kind == "TX":
                turn(("x", i, j), [xw[i][:, 2 * j, :], xw[i][:, 2 * j + 1, :]])
            elif kind == "CX":
                unturn(eng, ("x", i, j), xg[i][:, 1024 * j:1024 * (j + 1)])
            elif kind == "QX":
                quant(xc[i][:, 256 * j:256 * (j + 1)], xsc[i][:, 256 * j:256 * (j + 1)], xg[i][:, 1024 * j:1024 * (j + 1)])
            elif kind == "TF":
                turn(("f", i, j), [fr[i][:, 2 * j, :], fr[i][:, 2 * j + 1, :]])
            elif kind == "CF":
                unturn(eng, ("f", i, j), fg[i][:, 1024 * j:1024 * (j + 1)])
            elif kind == "QF":
                quant(fc[i][:, 256 * j:256 * (j + 1)], fsc[i][:, 256 * j:256 * (j + 1)], fg[i][:, 1024 * j:1024 * (j + 1)])
            elif kind == "MS":
                bank = take(("s", i, j))
                for r in range(2):
                    cols = slice((2 * j + r) * P, (2 * j + r + 1) * P)
                    nc.tensor.matmul_mx(out=bank[:, r * K:(r + 1) * K], lhsT=xc[i][:, cols].bitcast(FP8X4), lhsT_scale=xsc[i][:, cols],
                                        rhs=cc[i // 2][:].bitcast(FP8X4), rhs_scale=csc[i // 2][:], start=True, stop=True)
            elif kind == "B":
                bank = give(("s", i, j))
                nc.vector.scalar_tensor_tensor(out=tneg[i][:, 2 * j:2 * j + 2, :], in0=bank[:].rearrange("p (r n) -> p r n", r=2),
                                               scalar=-1.0 / math.sqrt(D), in1=bias[:].unsqueeze(1).to_broadcast([P, 2, K]),
                                               op0=ALU.mult, op1=ALU.subtract)
            elif kind == "X":
                nc.vector.tensor_reduce(out=mn[i][:, 2 * j:2 * j + 2], in_=tneg[i][:, 2 * j:2 * j + 2, :], axis=AX.X, op=ALU.min)
            elif kind == "E":
                nc.scalar.activation(out=ex[i][:, j, :], in_=tneg[i][:, j, :], func=ACT.Exp, scale=-1.0, bias=mn[i][:, j:j + 1],
                                     accum_out=sums[i][:, j:j + 1])
            elif kind == "R":
                nc.vector.reciprocal(out=rec[i][:], in_=sums[i][:])
            elif kind == "F":
                nc.vector.scalar_tensor_tensor(out=fac[i][:], in0=rec[i][:], scalar=float(K), in1=gt[:, i % 2, :], op0=ALU.mult, op1=ALU.mult)
            elif kind == "A":
                if eng == "g" and j == 1:
                    continue
                engine, lo, width = (nc.gpsimd, 0, K) if eng == "g" else (nc.vector, P * j, P)
                engine.tensor_tensor(out=ag[i][:, 4 * lo:4 * (lo + width)].rearrange("p (m t) -> p m t", t=4),
                                     in0=ex[i][:, :, lo:lo + width].rearrange("p t m -> p m t"),
                                     in1=fac[i][:].unsqueeze(1).to_broadcast([P, width, 4]), op=ALU.mult)
            elif kind == "QA":
                quant(ac[i][:, P * j:P * (j + 1)], asc[i][:, P * j:P * (j + 1)], ag[i][:, 512 * j:512 * (j + 1)])
            elif kind == "MV":
                bank = take(("v", i, j))
                for t in range(4):
                    cols = slice(t * P, (t + 1) * P)
                    nc.tensor.matmul_mx(out=bank[:, cols], lhsT=fc[i][:, cols].bitcast(FP8X4), lhsT_scale=fsc[i][:, cols],
                                        rhs=wv[:, 2 * P * j:2 * P * (j + 1)].bitcast(FP4X4), rhs_scale=wvs[:, P * j:P * (j + 1)],
                                        start=True, stop=True)
            elif kind == "CV":
                bank = give(("v", i, j))
                copy(eng, vg[i][:, 512 * j:512 * (j + 1)].rearrange("p (n t) -> p n t", t=4), bank[:].rearrange("p (t n) -> p n t", t=4))
            elif kind == "QV":
                quant(vc[i][:, 256 * j:256 * (j + 1)], vsc[i][:, 256 * j:256 * (j + 1)], vg[i][:, 1024 * j:1024 * (j + 1)])
            elif kind == "MU":
                first = i % 2 == 0
                bank = take(("u", i // 2, j)) if first else held[("u", i // 2, j)][1]
                cols = slice(j * P, (j + 1) * P)
                nc.tensor.matmul_mx(out=bank[:], lhsT=ac[i][:, cols].bitcast(FP8X4), lhsT_scale=asc[i][:, cols],
                                    rhs=vc[i][:].bitcast(FP8X4), rhs_scale=vsc[i][:], start=first, stop=not first)
            elif kind == "O":
                cols = slice(0, V) if len(nums) == 2 else slice(256 * nums[2], 256 * (nums[2] + 1))
                bank = give(("u", i, j)) if cols.stop == V else held[("u", i, j)][1]
                nc.vector.scalar_tensor_tensor(out=ot[2 * i + j][:, cols], in0=bank[:, cols], scalar=1.0 / math.sqrt(N), in1=ht[i][:, j, cols],
                                               op0=ALU.mult, op1=ALU.add)
            elif kind == "ST":
                cols = slice(0, V) if len(nums) == 2 else slice(256 * nums[2], 256 * (nums[2] + 1))
                nc.sync.dma_start(out=out[i].rearrange("(m j) v -> m j v", j=2)[:, j, cols], in_=ot[2 * i + j][:, cols])
